import numpy as np
import ml_dtypes


def mxq(x, axis, fmt="e4m3"):
    dtype, down = {"e4m3": (ml_dtypes.float8_e4m3fn, 7), "e5m2": (ml_dtypes.float8_e5m2, 14)}[fmt]
    v = np.moveaxis(np.asarray(x, np.float32).astype(ml_dtypes.bfloat16).astype(np.float64), axis, -1)
    blocks = v.reshape(v.shape[:-1] + (-1, 32))
    amax = np.abs(blocks).max(-1, keepdims=True)
    byte = np.maximum(np.where(amax > 0, np.frexp(amax)[1] - 1 + 127, 0) - down, 1)
    scale = np.exp2(byte - 127.0)
    codes = (blocks / scale).astype(np.float32).astype(dtype).astype(np.float64)
    return np.moveaxis((codes * scale).reshape(v.shape), -1, axis)


WIDE = False


def mx_kscale(k):
    if not WIDE:
        return np.ones(k)
    levels = np.array([10, -10, 5, -5, 0])
    if k % 512:
        return np.exp2(np.random.permutation(np.resize(levels, k // 32))).repeat(32)
    a = np.empty((k // 512, 16))
    for p in range(k // 512):
        a[p, :8] = np.random.permutation(np.resize(levels, 8))
        for g in range(8):
            far = levels[np.abs(levels - a[p, g]) >= 10]
            a[p, g + 8] = far[np.random.randint(len(far))]
    return np.exp2(a.ravel()).repeat(32)


def f64(x):
    return np.asarray(x).astype(np.float64)


def striped(idx):
    return np.tile(idx.reshape(-1, 16).T, (8, 1)).astype(np.uint16)


def unstriped(offs):
    return offs[:16].T.reshape(-1).astype(np.int64)


def pack_weight(w):
    k, n = w.shape
    w = f64(np.asarray(w, np.float32).astype(ml_dtypes.bfloat16)).reshape(k // 32, 32, n)
    amax = np.abs(w).max(1)
    byte = np.clip(np.where(amax > 0, np.frexp(amax)[1] - 1 + 127 - 7, 1), 1, 254)
    scaled = (w * np.exp2(127.0 - byte)[:, None, :]).reshape(k, n).astype(np.float32)
    words = np.ascontiguousarray(scaled.reshape(k // 512, 128, 4, n).transpose(0, 1, 3, 2)).astype(ml_dtypes.float8_e4m3fn).view(np.uint8)
    return words, np.ascontiguousarray(byte.astype(np.uint8).reshape(k // 512, 16, n))


def unpack_weight(words, scales):
    g, p, n, _ = words.shape
    vals = np.ascontiguousarray(words).view(ml_dtypes.float8_e4m3fn).astype(np.float64) * np.repeat(np.exp2(scales.astype(np.float64) - 127.0), 8, axis=1)[..., None]
    return vals.transpose(0, 1, 3, 2).reshape(g * 512, n)


def sigmoid(v):
    return 1.0 / (1.0 + np.exp(-np.maximum(v, -700.0)))


K, T, S, N = 1024, 2048, 1024, 256


def setup_inputs():
    n = np.random.standard_normal
    s = mx_kscale(K)[:, None]
    packed_xT = pack_weight(n((K, T)) * s)
    return {
        "x_words": packed_xT[0],
        "x_scales": packed_xT[1],
        "side": n((N, T)).astype(np.float32),
        "w1": (n((K, N)) / np.sqrt(K) / s).astype(np.float32),
        "offs": striped(np.random.permutation(T)[:S]),
    }


def reference(x_words, x_scales, side, w1, offs):
    xq = unpack_weight(x_words, x_scales)[:, unstriped(offs)]
    y = mxq(f64(w1), 0, "e4m3").T @ xq
    g = f64(side)[:, unstriped(offs)]
    return y * sigmoid(g)

@@ -1,0 +1,116 @@
+from contextlib import ExitStack
+
+import concourse.mybir as mybir
+
+K, T, S, N = 1024, 2048, 1024, 256
+FLOPS = 2 * K * N * S
+
+F32 = mybir.dt.float32
+BF16 = mybir.dt.bfloat16
+I32 = mybir.dt.int32
+U32 = mybir.dt.uint32
+U16 = mybir.dt.uint16
+U8 = mybir.dt.uint8
+FP8X4 = mybir.dt.float8_e4m3fn_x4
+SIGMOID = mybir.ActivationFunctionType.Sigmoid
+MULT = mybir.AluOpType.mult
+
+P = 128
+PACK = 4
+PASSES = K // (P * PACK)
+HALVES = N // P
+BANK = 512
+CHUNKS = S // BANK
+PIECES = [512, 256]
+
+
+def tile_picked_sidegate_sigmoid_p_kernel(tc, x_words, x_scales, side, w1, offs, out):
+    nc = tc.nc
+    with ExitStack() as ctx:
+        keep = ctx.enter_context(tc.tile_pool(name="keep", bufs=1))
+        psum = ctx.enter_context(tc.psum_pool(name="psum", bufs=1))
+
+        offsets = keep.tile([P, S // 16], U16, name="offsets")
+        word_table = [keep.tile([P, T], I32, name="word_table%d" % z, align_bytes=64) for z in range(PASSES)]
+        scale_table = keep.tile([P, T], U8, name="scale_table", align_bytes=64)
+        side_table = [keep.tile([P, T], F32, name="side_table%d" % h, align_bytes=64) for h in range(HALVES)]
+        w_raw = [keep.tile([P, PACK, N], F32, name="w_raw%d" % z, align_bytes=64) for z in range(PASSES)]
+
+        def entries(a, b):
+            return offsets[:, a // 16 : b // 16]
+
+        nc.gpsimd.memset(scale_table[:].bitcast(I32), 0)
+        for q in range(4):
+            nc.gpsimd.dma_start(
+                out=scale_table[32 * q : 32 * q + 4 * PASSES, :].bitcast(I32),
+                in_=x_scales[:, 4 * q : 4 * q + 4, :].bitcast(I32),
+            )
+        for z in range(PASSES):
+            nc.sync.dma_start(out=word_table[z][:], in_=x_words[z].rearrange("p c t -> p (c t)").bitcast(I32))
+            if z == 0:
+                nc.sync.dma_start(offsets[:], offs)
+            nc.sync.dma_start(
+                out=w_raw[z][:], in_=w1[z * P * PACK : (z + 1) * P * PACK, :].rearrange("(p j) n -> p j n", j=PACK)
+            )
+        for h in range(HALVES):
+            nc.sync.dma_start(out=side_table[h][:], in_=side[h * P : (h + 1) * P, :])
+
+        w_codes, w_scales = [], []
+
+        def quantise(z):
+            grouped = keep.tile([P, N, PACK], BF16, name="w_grouped%d" % z, align_bytes=64)
+            nc.scalar.copy(
+                out=grouped[:].rearrange("p (c i) t -> p c t i", i=4),
+                in_=w_raw[z][:].rearrange("p t (c i) -> p c t i", i=4),
+            )
+            codes = keep.tile([P, N], U32, name="w_codes%d" % z, align_bytes=64)
+            scales = keep.tile([P, N], U8, name="w_scales%d" % z, align_bytes=64)
+            nc.vector.quantize_mx(out=codes[:].bitcast(FP8X4), scales=scales[:], in_=grouped[:].rearrange("p n t -> p (n t)"))
+            w_codes.append(codes)
+            w_scales.append(scales)
+
+        def gather_words(z, c):
+            picked = keep.tile([P, BANK], U32, name="x_codes%d_%d" % (z, c), align_bytes=64)
+            nc.vector.tensor_copy(picked[:], word_table[z][:].bitcast(U32).indirect(entries(c * BANK, (c + 1) * BANK)))
+            return picked
+
+        def gather_scales(c):
+            picked = keep.tile([P, BANK], U8, name="x_planes%d" % c, align_bytes=64)
+            nc.vector.tensor_copy(picked[:], scale_table[:].indirect(entries(c * BANK, (c + 1) * BANK)))
+            return picked
+
+        banks = [[psum.tile([P, BANK], F32, name="acc%d_%d" % (h, c)) for c in range(CHUNKS)] for h in range(HALVES)]
+
+        def multiply(z, c, h, codes, planes):
+            nc.tensor.matmul_mx(
+                out=banks[h][c][:],
+                lhsT=w_codes[z][:, h * P : (h + 1) * P].bitcast(FP8X4),
+                lhsT_scale=w_scales[z][:, h * P : (h + 1) * P],
+                rhs=codes[:].bitcast(FP8X4),
+                rhs_scale=planes[4 * z : P, :],
+                start=(z == 0),
+                stop=(z == PASSES - 1),
+            )
+
+        x_codes0 = [gather_words(0, c) for c in range(CHUNKS)]
+        quantise(0)
+        x_planes = []
+        for c in range(CHUNKS):
+            x_planes.append(gather_scales(c))
+            for h in range(HALVES):
+                multiply(0, c, h, x_codes0[c], x_planes[c])
+        x_codes1 = [gather_words(1, 0)]
+        quantise(1)
+        x_codes1.append(gather_words(1, 1))
+        for h in range(HALVES):
+            for c in range(CHUNKS):
+                multiply(1, c, h, x_codes1[c], x_planes[c])
+
+        for h in range(HALVES):
+            width = PIECES[h]
+            for a in range(0, S, width):
+                gate = keep.tile([P, width], F32, name="gate%d_%d" % (h, a), align_bytes=64)
+                nc.scalar.activation(gate[:], side_table[h][:].indirect(entries(a, a + width)), SIGMOID)
+                result = keep.tile([P, width], F32, name="result%d_%d" % (h, a), align_bytes=64)
+                nc.vector.tensor_tensor(result[:], banks[h][a // BANK][:, a % BANK : a % BANK + width], gate[:], MULT)
+                nc.sync.dma_start(out=out[h * P : (h + 1) * P, a : a + width], in_=result[:])

@@ -21,7 +21,7 @@ PASSES = K // (P * PACK)
 HALVES = N // P
 BANK = 512
 CHUNKS = S // BANK
-PIECES = [512, 256]
+PIECES = [[(0, 512, False, (0, 512)), (512, 896, False, None), (896, 1024, False, (512, 1024))], [(512, 768, False, None), (768, 1024, False, (512, 1024)), (0, 384, True, (0, 384)), (384, 512, False, (384, 512))]]
 
 
 def tile_picked_sidegate_sigmoid_p_kernel(tc, x_words, x_scales, side, w1, offs, out):
@@ -39,21 +39,37 @@ def tile_picked_sidegate_sigmoid_p_kernel(tc, x_words, x_scales, side, w1, offs,
         def entries(a, b):
             return offsets[:, a // 16 : b // 16]
 
-        nc.gpsimd.memset(scale_table[:].bitcast(I32), 0)
-        for q in range(4):
-            nc.gpsimd.dma_start(
-                out=scale_table[32 * q : 32 * q + 4 * PASSES, :].bitcast(I32),
-                in_=x_scales[:, 4 * q : 4 * q + 4, :].bitcast(I32),
-            )
-        for z in range(PASSES):
-            nc.sync.dma_start(out=word_table[z][:], in_=x_words[z].rearrange("p c t -> p (c t)").bitcast(I32))
-            if z == 0:
-                nc.sync.dma_start(offsets[:], offs)
+        def load_w(z):
             nc.sync.dma_start(
                 out=w_raw[z][:], in_=w1[z * P * PACK : (z + 1) * P * PACK, :].rearrange("(p j) n -> p j n", j=PACK)
             )
-        for h in range(HALVES):
+
+        def load_words(z):
+            nc.sync.dma_start(out=word_table[z][:], in_=x_words[z].rearrange("p c t -> p (c t)").bitcast(I32))
+
+        def load_scales():
+            for q in range(4):
+                nc.sync.dma_start(
+                    out=scale_table[32 * q : 32 * q + 4 * PASSES, :].bitcast(I32),
+                    in_=x_scales[:, 4 * q : 4 * q + 4, :].bitcast(I32),
+                )
+
+        def load_side(h):
             nc.sync.dma_start(out=side_table[h][:], in_=side[h * P : (h + 1) * P, :])
+
+        nc.vector.memset(scale_table[:].bitcast(I32), 0)
+        warm_in = keep.tile([P, 1], F32, name="warm_in")
+        warm_out = keep.tile([P, 1], F32, name="warm_out")
+        nc.gpsimd.memset(warm_in[:], 0.0)
+        nc.scalar.activation(warm_out[:], warm_in[:], SIGMOID)
+        nc.sync.dma_start(offsets[:], offs)
+        load_words(0)
+        load_scales()
+        load_w(0)
+        load_w(1)
+        load_words(1)
+        load_side(0)
+        load_side(1)
 
         w_codes, w_scales = [], []
 
@@ -69,48 +85,50 @@ def tile_picked_sidegate_sigmoid_p_kernel(tc, x_words, x_scales, side, w1, offs,
             w_codes.append(codes)
             w_scales.append(scales)
 
-        def gather_words(z, c):
-            picked = keep.tile([P, BANK], U32, name="x_codes%d_%d" % (z, c), align_bytes=64)
-            nc.vector.tensor_copy(picked[:], word_table[z][:].bitcast(U32).indirect(entries(c * BANK, (c + 1) * BANK)))
-            return picked
-
-        def gather_scales(c):
-            picked = keep.tile([P, BANK], U8, name="x_planes%d" % c, align_bytes=64)
-            nc.vector.tensor_copy(picked[:], scale_table[:].indirect(entries(c * BANK, (c + 1) * BANK)))
+        def gather_words(z, a, b):
+            picked = keep.tile([P, b - a], U32, name="x_codes%d_%d" % (z, a), align_bytes=64)
+            nc.vector.tensor_copy(picked[:], word_table[z][:].bitcast(U32).indirect(entries(a, b)))
             return picked
 
         banks = [[psum.tile([P, BANK], F32, name="acc%d_%d" % (h, c)) for c in range(CHUNKS)] for h in range(HALVES)]
+        x_planes = keep.tile([P, S], U8, name="x_planes", align_bytes=64)
 
-        def multiply(z, c, h, codes, planes):
+        def multiply(z, c, h, codes):
             nc.tensor.matmul_mx(
                 out=banks[h][c][:],
                 lhsT=w_codes[z][:, h * P : (h + 1) * P].bitcast(FP8X4),
                 lhsT_scale=w_scales[z][:, h * P : (h + 1) * P],
-                rhs=codes[:].bitcast(FP8X4),
-                rhs_scale=planes[4 * z : P, :],
+                rhs=codes.bitcast(FP8X4),
+                rhs_scale=x_planes[4 * z : P, c * BANK : (c + 1) * BANK],
                 start=(z == 0),
                 stop=(z == PASSES - 1),
             )
 
-        x_codes0 = [gather_words(0, c) for c in range(CHUNKS)]
+        first = gather_words(0, 0, S)
+        nc.vector.tensor_copy(x_planes[:], scale_table[:].indirect(offsets[:]))
         quantise(0)
-        x_planes = []
-        for c in range(CHUNKS):
-            x_planes.append(gather_scales(c))
-            for h in range(HALVES):
-                multiply(0, c, h, x_codes0[c], x_planes[c])
-        x_codes1 = [gather_words(1, 0)]
         quantise(1)
-        x_codes1.append(gather_words(1, 1))
-        for h in range(HALVES):
-            for c in range(CHUNKS):
-                multiply(1, c, h, x_codes1[c], x_planes[c])
+        for c in range(CHUNKS):
+            for h in range(HALVES):
+                multiply(0, c, h, first[:, c * BANK : (c + 1) * BANK])
+        for c in range(CHUNKS):
+            second = gather_words(1, c * BANK, (c + 1) * BANK)
+            for h in range(HALVES):
+                multiply(1, c, h, second[:])
 
         for h in range(HALVES):
-            width = PIECES[h]
-            for a in range(0, S, width):
-                gate = keep.tile([P, width], F32, name="gate%d_%d" % (h, a), align_bytes=64)
-                nc.scalar.activation(gate[:], side_table[h][:].indirect(entries(a, a + width)), SIGMOID)
-                result = keep.tile([P, width], F32, name="result%d_%d" % (h, a), align_bytes=64)
-                nc.vector.tensor_tensor(result[:], banks[h][a // BANK][:, a % BANK : a % BANK + width], gate[:], MULT)
-                nc.sync.dma_start(out=out[h * P : (h + 1) * P, a : a + width], in_=result[:])
+            raw = {}
+            result = keep.tile([P, S], F32, name="result%d" % h, align_bytes=64)
+            for a, b, on_vector, store in PIECES[h]:
+                if on_vector:
+                    raw[a] = keep.tile([P, b - a], F32, name="raw%d_%d" % (h, a), align_bytes=64)
+                    nc.vector.tensor_copy(raw[a][:], side_table[h][:].indirect(entries(a, b)))
+            for a, b, on_vector, store in PIECES[h]:
+                gate = keep.tile([P, b - a], F32, name="gate%d_%d" % (h, a), align_bytes=64)
+                if on_vector:
+                    nc.scalar.activation(gate[:], raw[a][:], SIGMOID)
+                else:
+                    nc.scalar.activation(gate[:], side_table[h][:].indirect(entries(a, b)), SIGMOID)
+                nc.vector.tensor_tensor(result[:, a:b], banks[h][a // BANK][:, a % BANK : a % BANK + b - a], gate[:], MULT)
+                if store is not None:
+                    nc.sync.dma_start(out=out[h * P : (h + 1) * P, store[0] : store[1]], in_=result[:, store[0] : store[1]])

@@ -21,7 +21,8 @@ PASSES = K // (P * PACK)
 HALVES = N // P
 BANK = 512
 CHUNKS = S // BANK
-PIECES = [[(0, 512, False, (0, 512)), (512, 896, False, None), (896, 1024, False, (512, 1024))], [(512, 768, False, None), (768, 1024, False, (512, 1024)), (0, 384, True, (0, 384)), (384, 512, False, (384, 512))]]
+ON_VECTOR = 384
+PIECES = [[(512, 1024, (512, 1024)), (384, 512, None), (0, 384, (0, 512))], [(512, 768, None), (768, 1024, (512, 1024)), (384, 512, (384, 512)), (0, 256, (0, 256)), (256, 384, (256, 384))]]
 
 
 def tile_picked_sidegate_sigmoid_p_kernel(tc, x_words, x_scales, side, w1, offs, out):
@@ -62,8 +63,8 @@ def tile_picked_sidegate_sigmoid_p_kernel(tc, x_words, x_scales, side, w1, offs,
         warm_out = keep.tile([P, 1], F32, name="warm_out")
         nc.gpsimd.memset(warm_in[:], 0.0)
         nc.scalar.activation(warm_out[:], warm_in[:], SIGMOID)
-        nc.sync.dma_start(offsets[:], offs)
         load_words(0)
+        nc.sync.dma_start(offsets[:], offs)
         load_scales()
         load_w(0)
         load_w(1)
@@ -117,18 +118,13 @@ def tile_picked_sidegate_sigmoid_p_kernel(tc, x_words, x_scales, side, w1, offs,
                 multiply(1, c, h, second[:])
 
         for h in range(HALVES):
-            raw = {}
             result = keep.tile([P, S], F32, name="result%d" % h, align_bytes=64)
-            for a, b, on_vector, store in PIECES[h]:
-                if on_vector:
-                    raw[a] = keep.tile([P, b - a], F32, name="raw%d_%d" % (h, a), align_bytes=64)
-                    nc.vector.tensor_copy(raw[a][:], side_table[h][:].indirect(entries(a, b)))
-            for a, b, on_vector, store in PIECES[h]:
+            raw = keep.tile([P, ON_VECTOR], F32, name="raw%d" % h, align_bytes=64)
+            nc.vector.tensor_copy(raw[:], side_table[h][:].indirect(entries(0, ON_VECTOR)))
+            for a, b, store in PIECES[h]:
                 gate = keep.tile([P, b - a], F32, name="gate%d_%d" % (h, a), align_bytes=64)
-                if on_vector:
-                    nc.scalar.activation(gate[:], raw[a][:], SIGMOID)
-                else:
-                    nc.scalar.activation(gate[:], side_table[h][:].indirect(entries(a, b)), SIGMOID)
+                source = raw[:, a:b] if b <= ON_VECTOR else side_table[h][:].indirect(entries(a, b))
+                nc.scalar.activation(gate[:], source, SIGMOID)
                 nc.vector.tensor_tensor(result[:, a:b], banks[h][a // BANK][:, a % BANK : a % BANK + b - a], gate[:], MULT)
                 if store is not None:
                     nc.sync.dma_start(out=out[h * P : (h + 1) * P, store[0] : store[1]], in_=result[:, store[0] : store[1]])

@@ -17,12 +17,26 @@ MULT = mybir.AluOpType.mult
 
 P = 128
 PACK = 4
-PASSES = K // (P * PACK)
+K_PASS = P * PACK
+PASSES = K // K_PASS
 HALVES = N // P
+QUADRANT = 32
+PLANE_ROWS = 4
+LIST_ROWS = 16
 BANK = 512
 CHUNKS = S // BANK
-ON_VECTOR = 384
-PIECES = [[(512, 1024, (512, 1024)), (384, 512, None), (0, 384, (0, 512))], [(512, 768, None), (768, 1024, (512, 1024)), (384, 512, (384, 512)), (0, 256, (0, 256)), (256, 384, (256, 384))]]
+ALIGN = 64
+RUN = 4
+
+VECTOR_FIRST, VECTOR_LAST = 512, 768
+PIECES = [
+    [(0, 512), (768, 1024), (512, 768)],
+    [(0, 256), (256, 512), (768, 896), (512, 768), (896, 1024)],
+]
+STORES = [
+    {0: slice(0, 512), 512: slice(512, 1024)},
+    {256: slice(0, 512), 512: slice(512, 896), 896: slice(896, 1024)},
+]
 
 
 def tile_picked_sidegate_sigmoid_p_kernel(tc, x_words, x_scales, side, w1, offs, out):
@@ -31,100 +45,89 @@ def tile_picked_sidegate_sigmoid_p_kernel(tc, x_words, x_scales, side, w1, offs,
         keep = ctx.enter_context(tc.tile_pool(name="keep", bufs=1))
         psum = ctx.enter_context(tc.psum_pool(name="psum", bufs=1))
 
-        offsets = keep.tile([P, S // 16], U16, name="offsets")
-        word_table = [keep.tile([P, T], I32, name="word_table%d" % z, align_bytes=64) for z in range(PASSES)]
-        scale_table = keep.tile([P, T], U8, name="scale_table", align_bytes=64)
-        side_table = [keep.tile([P, T], F32, name="side_table%d" % h, align_bytes=64) for h in range(HALVES)]
-        w_raw = [keep.tile([P, PACK, N], F32, name="w_raw%d" % z, align_bytes=64) for z in range(PASSES)]
+        offsets = keep.tile([P, S // LIST_ROWS], U16, name="offsets")
+        word_table = [keep.tile([P, T], I32, name="word_table%d" % z, align_bytes=ALIGN) for z in range(PASSES)]
+        scale_table = keep.tile([P, T], U8, name="scale_table", align_bytes=ALIGN)
+        side_table = [keep.tile([P, T], F32, name="side_table%d" % h, align_bytes=ALIGN) for h in range(HALVES)]
+        w_raw = [keep.tile([P, PACK, N], F32, name="w_raw%d" % z, align_bytes=ALIGN) for z in range(PASSES)]
 
-        def entries(a, b):
-            return offsets[:, a // 16 : b // 16]
-
-        def load_w(z):
-            nc.sync.dma_start(
-                out=w_raw[z][:], in_=w1[z * P * PACK : (z + 1) * P * PACK, :].rearrange("(p j) n -> p j n", j=PACK)
-            )
+        def entries(first, last):
+            return offsets[:, first // LIST_ROWS : last // LIST_ROWS]
 
         def load_words(z):
             nc.sync.dma_start(out=word_table[z][:], in_=x_words[z].rearrange("p c t -> p (c t)").bitcast(I32))
 
-        def load_scales():
-            for q in range(4):
-                nc.sync.dma_start(
-                    out=scale_table[32 * q : 32 * q + 4 * PASSES, :].bitcast(I32),
-                    in_=x_scales[:, 4 * q : 4 * q + 4, :].bitcast(I32),
-                )
-
-        def load_side(h):
-            nc.sync.dma_start(out=side_table[h][:], in_=side[h * P : (h + 1) * P, :])
-
         nc.vector.memset(scale_table[:].bitcast(I32), 0)
-        warm_in = keep.tile([P, 1], F32, name="warm_in")
-        warm_out = keep.tile([P, 1], F32, name="warm_out")
-        nc.gpsimd.memset(warm_in[:], 0.0)
-        nc.scalar.activation(warm_out[:], warm_in[:], SIGMOID)
+
         load_words(0)
         nc.sync.dma_start(offsets[:], offs)
-        load_scales()
-        load_w(0)
-        load_w(1)
-        load_words(1)
-        load_side(0)
-        load_side(1)
-
-        w_codes, w_scales = [], []
-
-        def quantise(z):
-            grouped = keep.tile([P, N, PACK], BF16, name="w_grouped%d" % z, align_bytes=64)
-            nc.scalar.copy(
-                out=grouped[:].rearrange("p (c i) t -> p c t i", i=4),
-                in_=w_raw[z][:].rearrange("p t (c i) -> p c t i", i=4),
+        for q in range(P // QUADRANT):
+            nc.sync.dma_start(
+                out=scale_table[QUADRANT * q : QUADRANT * q + PLANE_ROWS * PASSES, :].bitcast(I32),
+                in_=x_scales[:, PLANE_ROWS * q : PLANE_ROWS * (q + 1), :].bitcast(I32),
             )
-            codes = keep.tile([P, N], U32, name="w_codes%d" % z, align_bytes=64)
-            scales = keep.tile([P, N], U8, name="w_scales%d" % z, align_bytes=64)
-            nc.vector.quantize_mx(out=codes[:].bitcast(FP8X4), scales=scales[:], in_=grouped[:].rearrange("p n t -> p (n t)"))
-            w_codes.append(codes)
-            w_scales.append(scales)
+        for z in range(PASSES):
+            rows = w1[z * K_PASS : (z + 1) * K_PASS, :]
+            nc.sync.dma_start(out=w_raw[z][:], in_=rows.rearrange("(p t) n -> p t n", t=PACK))
+        load_words(1)
+        for h in range(HALVES):
+            nc.sync.dma_start(out=side_table[h][:], in_=side[h * P : (h + 1) * P, :])
 
-        def gather_words(z, a, b):
-            picked = keep.tile([P, b - a], U32, name="x_codes%d_%d" % (z, a), align_bytes=64)
-            nc.vector.tensor_copy(picked[:], word_table[z][:].bitcast(U32).indirect(entries(a, b)))
+        def gather_words(z, first, last):
+            picked = keep.tile([P, last - first], U32, name="x_codes%d_%d" % (z, first), align_bytes=ALIGN)
+            nc.vector.tensor_copy(picked[:], word_table[z][:].bitcast(U32).indirect(entries(first, last)))
             return picked
 
-        banks = [[psum.tile([P, BANK], F32, name="acc%d_%d" % (h, c)) for c in range(CHUNKS)] for h in range(HALVES)]
-        x_planes = keep.tile([P, S], U8, name="x_planes", align_bytes=64)
+        x_codes0 = gather_words(0, 0, S)
+        x_planes = keep.tile([P, S], U8, name="x_planes", align_bytes=ALIGN)
+        nc.vector.tensor_copy(x_planes[:], scale_table[:].indirect(offsets[:]))
 
-        def multiply(z, c, h, codes):
-            nc.tensor.matmul_mx(
-                out=banks[h][c][:],
-                lhsT=w_codes[z][:, h * P : (h + 1) * P].bitcast(FP8X4),
-                lhsT_scale=w_scales[z][:, h * P : (h + 1) * P],
-                rhs=codes.bitcast(FP8X4),
-                rhs_scale=x_planes[4 * z : P, c * BANK : (c + 1) * BANK],
-                start=(z == 0),
-                stop=(z == PASSES - 1),
+        w_codes, w_plane = [], []
+        for z in range(PASSES):
+            grouped = keep.tile([P, N, PACK], BF16, name="w_grouped%d" % z, align_bytes=ALIGN)
+            nc.scalar.copy(
+                out=grouped[:].rearrange("p (c i) t -> p c t i", i=RUN),
+                in_=w_raw[z][:].rearrange("p t (c i) -> p c t i", i=RUN),
+            )
+            w_codes.append(keep.tile([P, N], U32, name="w_codes%d" % z, align_bytes=ALIGN))
+            w_plane.append(keep.tile([P, N], U8, name="w_plane%d" % z, align_bytes=ALIGN))
+            nc.vector.quantize_mx(
+                out=w_codes[z][:].bitcast(FP8X4), scales=w_plane[z][:], in_=grouped[:].rearrange("p n t -> p (n t)")
             )
 
-        first = gather_words(0, 0, S)
-        nc.vector.tensor_copy(x_planes[:], scale_table[:].indirect(offsets[:]))
-        quantise(0)
-        quantise(1)
-        for c in range(CHUNKS):
+        banks = [[psum.tile([P, BANK], F32, name="acc%d_%d" % (h, c)) for c in range(CHUNKS)] for h in range(HALVES)]
+
+        def multiply(z, c, codes):
             for h in range(HALVES):
-                multiply(0, c, h, first[:, c * BANK : (c + 1) * BANK])
+                columns = slice(h * P, (h + 1) * P)
+                nc.tensor.matmul_mx(
+                    out=banks[h][c][:],
+                    lhsT=w_codes[z][:, columns].bitcast(FP8X4),
+                    lhsT_scale=w_plane[z][:, columns],
+                    rhs=codes.bitcast(FP8X4),
+                    rhs_scale=x_planes[PLANE_ROWS * z : P, c * BANK : (c + 1) * BANK],
+                    start=(z == 0),
+                    stop=(z == PASSES - 1),
+                )
+
         for c in range(CHUNKS):
-            second = gather_words(1, c * BANK, (c + 1) * BANK)
-            for h in range(HALVES):
-                multiply(1, c, h, second[:])
+            multiply(0, c, x_codes0[:, c * BANK : (c + 1) * BANK])
+        for c in range(CHUNKS):
+            x_codes1 = gather_words(1, c * BANK, (c + 1) * BANK)
+            multiply(1, c, x_codes1[:])
 
         for h in range(HALVES):
-            result = keep.tile([P, S], F32, name="result%d" % h, align_bytes=64)
-            raw = keep.tile([P, ON_VECTOR], F32, name="raw%d" % h, align_bytes=64)
-            nc.vector.tensor_copy(raw[:], side_table[h][:].indirect(entries(0, ON_VECTOR)))
-            for a, b, store in PIECES[h]:
-                gate = keep.tile([P, b - a], F32, name="gate%d_%d" % (h, a), align_bytes=64)
-                source = raw[:, a:b] if b <= ON_VECTOR else side_table[h][:].indirect(entries(a, b))
-                nc.scalar.activation(gate[:], source, SIGMOID)
-                nc.vector.tensor_tensor(result[:, a:b], banks[h][a // BANK][:, a % BANK : a % BANK + b - a], gate[:], MULT)
-                if store is not None:
-                    nc.sync.dma_start(out=out[h * P : (h + 1) * P, store[0] : store[1]], in_=result[:, store[0] : store[1]])
+            result = keep.tile([P, S], F32, name="result%d" % h, align_bytes=ALIGN)
+            side_picked = keep.tile([P, VECTOR_LAST - VECTOR_FIRST], F32, name="side_picked%d" % h, align_bytes=ALIGN)
+            nc.vector.tensor_copy(side_picked[:], side_table[h][:].indirect(entries(VECTOR_FIRST, VECTOR_LAST)))
+            for first, last in PIECES[h]:
+                gate = keep.tile([P, last - first], F32, name="gate%d_%d" % (h, first), align_bytes=ALIGN)
+                if first == VECTOR_FIRST:
+                    nc.scalar.activation(gate[:], side_picked[:], SIGMOID)
+                else:
+                    nc.scalar.activation(gate[:], side_table[h][:].indirect(entries(first, last)), SIGMOID)
+                product = banks[h][first // BANK][:, first % BANK : first % BANK + last - first]
+                nc.vector.tensor_tensor(result[:, first:last], product, gate[:], MULT)
+                if first in STORES[h]:
+                    stored = STORES[h][first]
+                    nc.sync.dma_start(out=out[h * P : (h + 1) * P, stored], in_=result[:, stored])

@@ -26,6 +26,7 @@ LIST_ROWS = 16
 BANK = 512
 CHUNKS = S // BANK
 ALIGN = 64
+EARLY_SCALE_LOADS = 6
 RUN = 4
 
 VECTOR_FIRST, VECTOR_LAST = 512, 768
@@ -57,21 +58,34 @@ def tile_picked_sidegate_sigmoid_p_kernel(tc, x_words, x_scales, side, w1, offs,
         def load_words(z):
             nc.sync.dma_start(out=word_table[z][:], in_=x_words[z].rearrange("p c t -> p (c t)").bitcast(I32))
 
-        nc.vector.memset(scale_table[:].bitcast(I32), 0)
-
-        load_words(0)
-        nc.sync.dma_start(offsets[:], offs)
-        for q in range(P // QUADRANT):
+        def load_scales(r, z):
             nc.sync.dma_start(
-                out=scale_table[QUADRANT * q : QUADRANT * q + PLANE_ROWS * PASSES, :].bitcast(I32),
-                in_=x_scales[:, PLANE_ROWS * q : PLANE_ROWS * (q + 1), :].bitcast(I32),
+                out=scale_table[PLANE_ROWS * z + r : P : QUADRANT, :].bitcast(I32),
+                in_=x_scales[z, r : PLANE_ROWS * PLANE_ROWS : PLANE_ROWS, :].bitcast(I32),
             )
-        for z in range(PASSES):
+
+        def load_weights(z):
             rows = w1[z * K_PASS : (z + 1) * K_PASS, :]
             nc.sync.dma_start(out=w_raw[z][:], in_=rows.rearrange("(p t) n -> p t n", t=PACK))
+
+        nc.vector.memset(scale_table[:].bitcast(I32), 0)
+
+        nc.sync.dma_start(offsets[:], offs)
+        load_words(0)
+        scale_rows = [(r, z) for r in range(PLANE_ROWS) for z in range(PASSES)]
+        for r, z in scale_rows[:EARLY_SCALE_LOADS]:
+            load_scales(r, z)
+        load_weights(0)
+        for r, z in scale_rows[EARLY_SCALE_LOADS:]:
+            load_scales(r, z)
+        load_weights(1)
         load_words(1)
         for h in range(HALVES):
             nc.sync.dma_start(out=side_table[h][:], in_=side[h * P : (h + 1) * P, :])
+
+        warm = keep.tile([P, 8], F32, name="warm")
+        nc.gpsimd.memset(warm[:, 0:4], 0.0)
+        nc.scalar.activation(warm[:, 4:5], warm[:, 0:1], SIGMOID)
 
         def gather_words(z, first, last):
             picked = keep.tile([P, last - first], U32, name="x_codes%d_%d" % (z, first), align_bytes=ALIGN)

@@ -26,17 +26,18 @@ LIST_ROWS = 16
 BANK = 512
 CHUNKS = S // BANK
 ALIGN = 64
-EARLY_SCALE_LOADS = 6
 RUN = 4
+SCALE_ROWS = PASSES * PLANE_ROWS * PLANE_ROWS
+EARLY_MOVES = 5
 
-VECTOR_FIRST, VECTOR_LAST = 512, 768
+VECTOR_SHARE = [(640, 1024), (704, 1024)]
 PIECES = [
-    [(0, 512), (768, 1024), (512, 768)],
-    [(0, 256), (256, 512), (768, 896), (512, 768), (896, 1024)],
+    [(0, 256), (256, 512), (640, 896), (896, 1024), (512, 640)],
+    [(0, 256), (256, 512), (704, 1024), (512, 608), (608, 704)],
 ]
 STORES = [
-    {0: slice(0, 512), 512: slice(512, 1024)},
-    {256: slice(0, 512), 512: slice(512, 896), 896: slice(896, 1024)},
+    {256: slice(0, 512), 512: slice(512, 1024)},
+    {0: slice(0, 256), 256: slice(256, 512), 704: slice(704, 1024), 608: slice(512, 704)},
 ]
 
 
@@ -44,13 +45,25 @@ def tile_picked_sidegate_sigmoid_p_kernel(tc, x_words, x_scales, side, w1, offs,
     nc = tc.nc
     with ExitStack() as ctx:
         keep = ctx.enter_context(tc.tile_pool(name="keep", bufs=1))
+        reused = ctx.enter_context(tc.tile_pool(name="reused", bufs=1))
         psum = ctx.enter_context(tc.psum_pool(name="psum", bufs=1))
 
         offsets = keep.tile([P, S // LIST_ROWS], U16, name="offsets")
-        word_table = [keep.tile([P, T], I32, name="word_table%d" % z, align_bytes=ALIGN) for z in range(PASSES)]
-        scale_table = keep.tile([P, T], U8, name="scale_table", align_bytes=ALIGN)
-        side_table = [keep.tile([P, T], F32, name="side_table%d" % h, align_bytes=ALIGN) for h in range(HALVES)]
-        w_raw = [keep.tile([P, PACK, N], F32, name="w_raw%d" % z, align_bytes=ALIGN) for z in range(PASSES)]
+        scale_table = reused.tile([P, T], U8, name="scale_table", align_bytes=ALIGN, offset=3072)
+        word_table = [
+            reused.tile([P, T], I32, name="word_table0", align_bytes=ALIGN, offset=12288),
+            keep.tile([P, T], I32, name="word_table1", align_bytes=ALIGN),
+        ]
+        w_raw = [
+            keep.tile([P, PACK, N], F32, name="w_raw0", align_bytes=ALIGN),
+            reused.tile([P, PACK, N], F32, name="w_raw1", align_bytes=ALIGN, offset=0),
+        ]
+        side_table = [
+            reused.tile([P, T], F32, name="side_table0", align_bytes=ALIGN, offset=4096),
+            reused.tile([P, T], F32, name="side_table1", align_bytes=ALIGN, offset=12288),
+        ]
+        scales_picked = keep.tile([P, S], U8, name="scales_picked", align_bytes=ALIGN)
+        x_planes = [keep.tile([P, S], U8, name="x_plane%d" % z, align_bytes=ALIGN) for z in range(PASSES)]
 
         def entries(first, last):
             return offsets[:, first // LIST_ROWS : last // LIST_ROWS]
@@ -58,86 +71,63 @@ def tile_picked_sidegate_sigmoid_p_kernel(tc, x_words, x_scales, side, w1, offs,
         def load_words(z):
             nc.sync.dma_start(out=word_table[z][:], in_=x_words[z].rearrange("p c t -> p (c t)").bitcast(I32))
 
-        def load_scales(r, z):
-            nc.sync.dma_start(
-                out=scale_table[PLANE_ROWS * z + r : P : QUADRANT, :].bitcast(I32),
-                in_=x_scales[z, r : PLANE_ROWS * PLANE_ROWS : PLANE_ROWS, :].bitcast(I32),
-            )
-
         def load_weights(z):
             rows = w1[z * K_PASS : (z + 1) * K_PASS, :]
             nc.sync.dma_start(out=w_raw[z][:], in_=rows.rearrange("(p t) n -> p t n", t=PACK))
 
-        nc.vector.memset(scale_table[:].bitcast(I32), 0)
-
-        nc.sync.dma_start(offsets[:], offs)
-        load_words(0)
-        scale_rows = [(r, z) for r in range(PLANE_ROWS) for z in range(PASSES)]
-        for r, z in scale_rows[:EARLY_SCALE_LOADS]:
-            load_scales(r, z)
-        load_weights(0)
-        for r, z in scale_rows[EARLY_SCALE_LOADS:]:
-            load_scales(r, z)
-        load_weights(1)
-        load_words(1)
-        for h in range(HALVES):
+        def load_side(h):
             nc.sync.dma_start(out=side_table[h][:], in_=side[h * P : (h + 1) * P, :])
 
-        warm = keep.tile([P, 8], F32, name="warm")
-        nc.gpsimd.memset(warm[:, 0:4], 0.0)
-        nc.scalar.activation(warm[:, 4:5], warm[:, 0:1], SIGMOID)
+        def move_scales(z, r):
+            first = SCALE_ROWS // PASSES * z + r
+            nc.sync.dma_start(
+                out=x_planes[z][PLANE_ROWS * z + r : P : QUADRANT, :].bitcast(I32),
+                in_=scales_picked[first : first + SCALE_ROWS // PASSES - r : PLANE_ROWS, :].bitcast(I32),
+            )
 
         def gather_words(z, first, last):
             picked = keep.tile([P, last - first], U32, name="x_codes%d_%d" % (z, first), align_bytes=ALIGN)
             nc.vector.tensor_copy(picked[:], word_table[z][:].bitcast(U32).indirect(entries(first, last)))
             return picked
 
-        x_codes0 = gather_words(0, 0, S)
-        x_planes = keep.tile([P, S], U8, name="x_planes", align_bytes=ALIGN)
-        nc.vector.tensor_copy(x_planes[:], scale_table[:].indirect(offsets[:]))
-
-        w_codes, w_plane = [], []
-        for z in range(PASSES):
-            grouped = keep.tile([P, N, PACK], BF16, name="w_grouped%d" % z, align_bytes=ALIGN)
-            nc.scalar.copy(
+        def round_weights(copy, z, first, last):
+            grouped = keep.tile([P, last - first, PACK], BF16, name="w_grouped%d_%d" % (z, first), align_bytes=ALIGN)
+            copy(
                 out=grouped[:].rearrange("p (c i) t -> p c t i", i=RUN),
-                in_=w_raw[z][:].rearrange("p t (c i) -> p c t i", i=RUN),
+                in_=w_raw[z][:, :, first:last].rearrange("p t (c i) -> p c t i", i=RUN),
             )
-            w_codes.append(keep.tile([P, N], U32, name="w_codes%d" % z, align_bytes=ALIGN))
-            w_plane.append(keep.tile([P, N], U8, name="w_plane%d" % z, align_bytes=ALIGN))
-            nc.vector.quantize_mx(
-                out=w_codes[z][:].bitcast(FP8X4), scales=w_plane[z][:], in_=grouped[:].rearrange("p n t -> p (n t)")
-            )
+            return grouped
+
+        def quantise_weights(grouped, z, first, last):
+            codes = keep.tile([P, last - first], U32, name="w_codes%d_%d" % (z, first), align_bytes=ALIGN)
+            plane = keep.tile([P, last - first], U8, name="w_plane%d_%d" % (z, first), align_bytes=ALIGN)
+            nc.vector.quantize_mx(out=codes[:].bitcast(FP8X4), scales=plane[:], in_=grouped[:].rearrange("p n t -> p (n t)"))
+            return codes, plane
 
         banks = [[psum.tile([P, BANK], F32, name="acc%d_%d" % (h, c)) for c in range(CHUNKS)] for h in range(HALVES)]
 
-        def multiply(z, c, codes):
+        def multiply(z, w_codes, w_plane, x_codes):
             for h in range(HALVES):
-                columns = slice(h * P, (h + 1) * P)
-                nc.tensor.matmul_mx(
-                    out=banks[h][c][:],
-                    lhsT=w_codes[z][:, columns].bitcast(FP8X4),
-                    lhsT_scale=w_plane[z][:, columns],
-                    rhs=codes.bitcast(FP8X4),
-                    rhs_scale=x_planes[PLANE_ROWS * z : P, c * BANK : (c + 1) * BANK],
-                    start=(z == 0),
-                    stop=(z == PASSES - 1),
-                )
+                for c in range(CHUNKS):
+                    nc.tensor.matmul_mx(
+                        out=banks[h][c][:],
+                        lhsT=w_codes[:, h * P : (h + 1) * P].bitcast(FP8X4),
+                        lhsT_scale=w_plane[:, h * P : (h + 1) * P],
+                        rhs=x_codes[:, c * BANK : (c + 1) * BANK].bitcast(FP8X4),
+                        rhs_scale=x_planes[z][PLANE_ROWS * z : P, c * BANK : (c + 1) * BANK],
+                        start=(z == 0),
+                        stop=(z == PASSES - 1),
+                    )
 
-        for c in range(CHUNKS):
-            multiply(0, c, x_codes0[:, c * BANK : (c + 1) * BANK])
-        for c in range(CHUNKS):
-            x_codes1 = gather_words(1, c * BANK, (c + 1) * BANK)
-            multiply(1, c, x_codes1[:])
-
-        for h in range(HALVES):
+        def finish(h):
             result = keep.tile([P, S], F32, name="result%d" % h, align_bytes=ALIGN)
-            side_picked = keep.tile([P, VECTOR_LAST - VECTOR_FIRST], F32, name="side_picked%d" % h, align_bytes=ALIGN)
-            nc.vector.tensor_copy(side_picked[:], side_table[h][:].indirect(entries(VECTOR_FIRST, VECTOR_LAST)))
+            share_first, share_last = VECTOR_SHARE[h]
+            picked = keep.tile([P, share_last - share_first], F32, name="side_picked%d" % h, align_bytes=ALIGN)
+            nc.vector.tensor_copy(picked[:], side_table[h][:].indirect(entries(share_first, share_last)))
             for first, last in PIECES[h]:
                 gate = keep.tile([P, last - first], F32, name="gate%d_%d" % (h, first), align_bytes=ALIGN)
-                if first == VECTOR_FIRST:
-                    nc.scalar.activation(gate[:], side_picked[:], SIGMOID)
+                if share_first <= first < share_last:
+                    nc.scalar.activation(gate[:], picked[:, first - share_first : last - share_first], SIGMOID)
                 else:
                     nc.scalar.activation(gate[:], side_table[h][:].indirect(entries(first, last)), SIGMOID)
                 product = banks[h][first // BANK][:, first % BANK : first % BANK + last - first]
@@ -145,3 +135,35 @@ def tile_picked_sidegate_sigmoid_p_kernel(tc, x_words, x_scales, side, w1, offs,
                 if first in STORES[h]:
                     stored = STORES[h][first]
                     nc.sync.dma_start(out=out[h * P : (h + 1) * P, stored], in_=result[:, stored])
+            return result
+
+        nc.vector.memset(scale_table[32:64, :].bitcast(I32), 0)
+        nc.vector.memset(scale_table[64:128, :].bitcast(I32), 0)
+        nc.sync.dma_start(offsets[:], offs)
+        nc.sync.dma_start(out=scale_table[0:SCALE_ROWS, :].bitcast(I32), in_=x_scales.rearrange("z q c -> (z q) c").bitcast(I32))
+        load_words(0)
+        load_weights(0)
+        load_words(1)
+
+        warm = keep.tile([P, 8], F32, name="warm")
+        nc.gpsimd.memset(warm[:, 0:4], 0.0)
+        nc.scalar.activation(warm[:, 4:5], warm[:, 0:1], SIGMOID)
+
+        nc.vector.tensor_copy(scales_picked[:], scale_table[:].indirect(offsets[:]))
+        x_codes0 = gather_words(0, 0, S)
+        moves = [(z, r) for z in range(PASSES) for r in range(PLANE_ROWS)]
+        for z, r in moves[:EARLY_MOVES]:
+            move_scales(z, r)
+        load_weights(1)
+        load_side(0)
+        for z, r in moves[EARLY_MOVES:]:
+            move_scales(z, r)
+        load_side(1)
+
+        codes0, plane0 = quantise_weights(round_weights(nc.scalar.copy, 0, 0, N), 0, 0, N)
+        x_codes1 = gather_words(1, 0, S)
+        codes1, plane1 = quantise_weights(round_weights(nc.scalar.copy, 1, 0, N), 1, 0, N)
+        multiply(0, codes0, plane0, x_codes0)
+        multiply(1, codes1, plane1, x_codes1)
+        for h in range(HALVES):
+            finish(h)

@@ -28,7 +28,7 @@ CHUNKS = S // BANK
 ALIGN = 64
 RUN = 4
 SCALE_ROWS = PASSES * PLANE_ROWS * PLANE_ROWS
-EARLY_MOVES = 5
+EARLY_MOVES = 4
 
 VECTOR_SHARE = [(640, 1024), (704, 1024)]
 PIECES = [
@@ -139,8 +139,8 @@ def tile_picked_sidegate_sigmoid_p_kernel(tc, x_words, x_scales, side, w1, offs,
 
         nc.vector.memset(scale_table[32:64, :].bitcast(I32), 0)
         nc.vector.memset(scale_table[64:128, :].bitcast(I32), 0)
-        nc.sync.dma_start(offsets[:], offs)
         nc.sync.dma_start(out=scale_table[0:SCALE_ROWS, :].bitcast(I32), in_=x_scales.rearrange("z q c -> (z q) c").bitcast(I32))
+        nc.sync.dma_start(offsets[:], offs)
         load_words(0)
         load_weights(0)
         load_words(1)

@@ -22,13 +22,17 @@ PASSES = K // K_PASS
 HALVES = N // P
 QUADRANT = 32
 PLANE_ROWS = 4
+PASS_ROWS = PLANE_ROWS * P // QUADRANT
 LIST_ROWS = 16
 BANK = 512
 CHUNKS = S // BANK
 ALIGN = 64
 RUN = 4
-SCALE_ROWS = PASSES * PLANE_ROWS * PLANE_ROWS
-EARLY_MOVES = 4
+
+W_LATE_AT = 0
+SIDE0_AT = PACK * N * 4
+SCALE_TABLE_AT = SIDE0_AT - T // 2
+WORDS0_AT = SIDE0_AT + T * 4
 
 VECTOR_SHARE = [(640, 1024), (704, 1024)]
 PIECES = [
@@ -49,18 +53,18 @@ def tile_picked_sidegate_sigmoid_p_kernel(tc, x_words, x_scales, side, w1, offs,
         psum = ctx.enter_context(tc.psum_pool(name="psum", bufs=1))
 
         offsets = keep.tile([P, S // LIST_ROWS], U16, name="offsets")
-        scale_table = reused.tile([P, T], U8, name="scale_table", align_bytes=ALIGN, offset=3072)
+        scale_table = reused.tile([P, T], U8, name="scale_table", align_bytes=ALIGN, offset=SCALE_TABLE_AT)
         word_table = [
-            reused.tile([P, T], I32, name="word_table0", align_bytes=ALIGN, offset=12288),
+            reused.tile([P, T], I32, name="word_table0", align_bytes=ALIGN, offset=WORDS0_AT),
             keep.tile([P, T], I32, name="word_table1", align_bytes=ALIGN),
         ]
         w_raw = [
             keep.tile([P, PACK, N], F32, name="w_raw0", align_bytes=ALIGN),
-            reused.tile([P, PACK, N], F32, name="w_raw1", align_bytes=ALIGN, offset=0),
+            reused.tile([P, PACK, N], F32, name="w_raw1", align_bytes=ALIGN, offset=W_LATE_AT),
         ]
         side_table = [
-            reused.tile([P, T], F32, name="side_table0", align_bytes=ALIGN, offset=4096),
-            reused.tile([P, T], F32, name="side_table1", align_bytes=ALIGN, offset=12288),
+            reused.tile([P, T], F32, name="side_table0", align_bytes=ALIGN, offset=SIDE0_AT),
+            reused.tile([P, T], F32, name="side_table1", align_bytes=ALIGN, offset=WORDS0_AT),
         ]
         scales_picked = keep.tile([P, S], U8, name="scales_picked", align_bytes=ALIGN)
         x_planes = [keep.tile([P, S], U8, name="x_plane%d" % z, align_bytes=ALIGN) for z in range(PASSES)]
@@ -78,29 +82,26 @@ def tile_picked_sidegate_sigmoid_p_kernel(tc, x_words, x_scales, side, w1, offs,
         def load_side(h):
             nc.sync.dma_start(out=side_table[h][:], in_=side[h * P : (h + 1) * P, :])
 
-        def move_scales(z, r):
-            first = SCALE_ROWS // PASSES * z + r
-            nc.sync.dma_start(
-                out=x_planes[z][PLANE_ROWS * z + r : P : QUADRANT, :].bitcast(I32),
-                in_=scales_picked[first : first + SCALE_ROWS // PASSES - r : PLANE_ROWS, :].bitcast(I32),
-            )
+        def move_scales(z):
+            for r in range(PLANE_ROWS):
+                nc.sync.dma_start(
+                    out=x_planes[z][PLANE_ROWS * z + r : P : QUADRANT, :].bitcast(I32),
+                    in_=scales_picked[PASS_ROWS * z + r : PASS_ROWS * (z + 1) : PLANE_ROWS, :].bitcast(I32),
+                )
 
-        def gather_words(z, first, last):
-            picked = keep.tile([P, last - first], U32, name="x_codes%d_%d" % (z, first), align_bytes=ALIGN)
-            nc.vector.tensor_copy(picked[:], word_table[z][:].bitcast(U32).indirect(entries(first, last)))
+        def gather_words(z):
+            picked = keep.tile([P, S], U32, name="x_codes%d" % z, align_bytes=ALIGN)
+            nc.vector.tensor_copy(picked[:], word_table[z][:].bitcast(U32).indirect(offsets[:]))
             return picked
 
-        def round_weights(copy, z, first, last):
-            grouped = keep.tile([P, last - first, PACK], BF16, name="w_grouped%d_%d" % (z, first), align_bytes=ALIGN)
-            copy(
+        def quantise_weights(z):
+            grouped = keep.tile([P, N, PACK], BF16, name="w_grouped%d" % z, align_bytes=ALIGN)
+            nc.scalar.copy(
                 out=grouped[:].rearrange("p (c i) t -> p c t i", i=RUN),
-                in_=w_raw[z][:, :, first:last].rearrange("p t (c i) -> p c t i", i=RUN),
+                in_=w_raw[z][:].rearrange("p t (c i) -> p c t i", i=RUN),
             )
-            return grouped
-
-        def quantise_weights(grouped, z, first, last):
-            codes = keep.tile([P, last - first], U32, name="w_codes%d_%d" % (z, first), align_bytes=ALIGN)
-            plane = keep.tile([P, last - first], U8, name="w_plane%d_%d" % (z, first), align_bytes=ALIGN)
+            codes = keep.tile([P, N], U32, name="w_codes%d" % z, align_bytes=ALIGN)
+            plane = keep.tile([P, N], U8, name="w_plane%d" % z, align_bytes=ALIGN)
             nc.vector.quantize_mx(out=codes[:].bitcast(FP8X4), scales=plane[:], in_=grouped[:].rearrange("p n t -> p (n t)"))
             return codes, plane
 
@@ -122,12 +123,12 @@ def tile_picked_sidegate_sigmoid_p_kernel(tc, x_words, x_scales, side, w1, offs,
         def finish(h):
             result = keep.tile([P, S], F32, name="result%d" % h, align_bytes=ALIGN)
             share_first, share_last = VECTOR_SHARE[h]
-            picked = keep.tile([P, share_last - share_first], F32, name="side_picked%d" % h, align_bytes=ALIGN)
-            nc.vector.tensor_copy(picked[:], side_table[h][:].indirect(entries(share_first, share_last)))
+            side_picked = keep.tile([P, share_last - share_first], F32, name="side_picked%d" % h, align_bytes=ALIGN)
+            nc.vector.tensor_copy(side_picked[:], side_table[h][:].indirect(entries(share_first, share_last)))
             for first, last in PIECES[h]:
                 gate = keep.tile([P, last - first], F32, name="gate%d_%d" % (h, first), align_bytes=ALIGN)
-                if share_first <= first < share_last:
-                    nc.scalar.activation(gate[:], picked[:, first - share_first : last - share_first], SIGMOID)
+                if first >= share_first:
+                    nc.scalar.activation(gate[:], side_picked[:, first - share_first : last - share_first], SIGMOID)
                 else:
                     nc.scalar.activation(gate[:], side_table[h][:].indirect(entries(first, last)), SIGMOID)
                 product = banks[h][first // BANK][:, first % BANK : first % BANK + last - first]
@@ -135,35 +136,34 @@ def tile_picked_sidegate_sigmoid_p_kernel(tc, x_words, x_scales, side, w1, offs,
                 if first in STORES[h]:
                     stored = STORES[h][first]
                     nc.sync.dma_start(out=out[h * P : (h + 1) * P, stored], in_=result[:, stored])
-            return result
 
-        nc.vector.memset(scale_table[32:64, :].bitcast(I32), 0)
-        nc.vector.memset(scale_table[64:128, :].bitcast(I32), 0)
-        nc.sync.dma_start(out=scale_table[0:SCALE_ROWS, :].bitcast(I32), in_=x_scales.rearrange("z q c -> (z q) c").bitcast(I32))
+        nc.vector.memset(scale_table[QUADRANT : 2 * QUADRANT, :].bitcast(I32), 0)
+        nc.vector.memset(scale_table[2 * QUADRANT : P, :].bitcast(I32), 0)
+        nc.sync.dma_start(
+            out=scale_table[0 : PASSES * PASS_ROWS, :].bitcast(I32),
+            in_=x_scales.rearrange("z g c -> (z g) c").bitcast(I32),
+        )
         nc.sync.dma_start(offsets[:], offs)
         load_words(0)
         load_weights(0)
         load_words(1)
 
         warm = keep.tile([P, 8], F32, name="warm")
-        nc.gpsimd.memset(warm[:, 0:4], 0.0)
+        nc.vector.memset(warm[:, 0:4], 0.0)
         nc.scalar.activation(warm[:, 4:5], warm[:, 0:1], SIGMOID)
 
         nc.vector.tensor_copy(scales_picked[:], scale_table[:].indirect(offsets[:]))
-        x_codes0 = gather_words(0, 0, S)
-        moves = [(z, r) for z in range(PASSES) for r in range(PLANE_ROWS)]
-        for z, r in moves[:EARLY_MOVES]:
-            move_scales(z, r)
+        x_codes0 = gather_words(0)
+        move_scales(0)
         load_weights(1)
         load_side(0)
-        for z, r in moves[EARLY_MOVES:]:
-            move_scales(z, r)
+        move_scales(1)
         load_side(1)
 
-        codes0, plane0 = quantise_weights(round_weights(nc.scalar.copy, 0, 0, N), 0, 0, N)
-        x_codes1 = gather_words(1, 0, S)
-        codes1, plane1 = quantise_weights(round_weights(nc.scalar.copy, 1, 0, N), 1, 0, N)
-        multiply(0, codes0, plane0, x_codes0)
-        multiply(1, codes1, plane1, x_codes1)
+        w_codes0, w_plane0 = quantise_weights(0)
+        x_codes1 = gather_words(1)
+        w_codes1, w_plane1 = quantise_weights(1)
+        multiply(0, w_codes0, w_plane0, x_codes0)
+        multiply(1, w_codes1, w_plane1, x_codes1)
         for h in range(HALVES):
             finish(h)

@@ -75,9 +75,9 @@ def tile_picked_sidegate_sigmoid_p_kernel(tc, x_words, x_scales, side, w1, offs,
         def load_words(z):
             nc.sync.dma_start(out=word_table[z][:], in_=x_words[z].rearrange("p c t -> p (c t)").bitcast(I32))
 
-        def load_weights(z):
+        def load_weights(z, partitions=slice(0, P)):
             rows = w1[z * K_PASS : (z + 1) * K_PASS, :]
-            nc.sync.dma_start(out=w_raw[z][:], in_=rows.rearrange("(p t) n -> p t n", t=PACK))
+            nc.sync.dma_start(out=w_raw[z][partitions], in_=rows.rearrange("(p t) n -> p t n", t=PACK)[partitions])
 
         def load_side(h):
             nc.sync.dma_start(out=side_table[h][:], in_=side[h * P : (h + 1) * P, :])
@@ -139,13 +139,15 @@ def tile_picked_sidegate_sigmoid_p_kernel(tc, x_words, x_scales, side, w1, offs,
 
         nc.vector.memset(scale_table[QUADRANT : 2 * QUADRANT, :].bitcast(I32), 0)
         nc.vector.memset(scale_table[2 * QUADRANT : P, :].bitcast(I32), 0)
+        load_weights(0, slice(0, P, 4))
         nc.sync.dma_start(
             out=scale_table[0 : PASSES * PASS_ROWS, :].bitcast(I32),
             in_=x_scales.rearrange("z g c -> (z g) c").bitcast(I32),
         )
         nc.sync.dma_start(offsets[:], offs)
         load_words(0)
-        load_weights(0)
+        load_weights(0, slice(1, P, 2))
+        load_weights(0, slice(2, P, 4))
         load_words(1)
 
         warm = keep.tile([P, 8], F32, name="warm")

@@ -41,7 +41,7 @@ PIECES = [
 ]
 STORES = [
     {256: slice(0, 512), 512: slice(512, 1024)},
-    {0: slice(0, 256), 256: slice(256, 512), 704: slice(704, 1024), 608: slice(512, 704)},
+    {0: slice(0, 256), 256: slice(256, 512), 704: slice(768, 1024), 608: slice(512, 768)},
 ]
 
 

@@ -26,7 +26,7 @@ PASS_ROWS = PLANE_ROWS * P // QUADRANT
 LIST_ROWS = 16
 BANK = 512
 CHUNKS = S // BANK
-ALIGN = 64
+ALIGN = 256
 RUN = 4
 
 W_LATE_AT = 0

@@ -34,14 +34,14 @@ SIDE0_AT = PACK * N * 4
 SCALE_TABLE_AT = SIDE0_AT - T // 2
 WORDS0_AT = SIDE0_AT + T * 4
 
-VECTOR_SHARE = [(640, 1024), (704, 1024)]
+VECTOR_SHARE = [(576, 1024), (640, 1024)]
 PIECES = [
-    [(0, 256), (256, 512), (640, 896), (896, 1024), (512, 640)],
-    [(0, 256), (256, 512), (704, 1024), (512, 608), (608, 704)],
+    [(0, 256), (256, 512), (576, 832), (832, 1024), (512, 576)],
+    [(0, 256), (256, 512), (640, 832), (832, 1024), (512, 640)],
 ]
 STORES = [
-    {256: slice(0, 512), 512: slice(512, 1024)},
-    {0: slice(0, 256), 256: slice(256, 512), 704: slice(768, 1024), 608: slice(512, 768)},
+    {512: slice(0, 1024)},
+    {0: slice(0, 256), 256: slice(256, 512), 640: slice(640, 832), 832: slice(832, 1024), 512: slice(512, 640)},
 ]
 
 

from contextlib import ExitStack

import concourse.mybir as mybir

K, T, S, N = 1024, 2048, 1024, 256
FLOPS = 2 * K * N * S

F32 = mybir.dt.float32
BF16 = mybir.dt.bfloat16
I32 = mybir.dt.int32
U32 = mybir.dt.uint32
U16 = mybir.dt.uint16
U8 = mybir.dt.uint8
FP8X4 = mybir.dt.float8_e4m3fn_x4
SIGMOID = mybir.ActivationFunctionType.Sigmoid
MULT = mybir.AluOpType.mult

P = 128
PACK = 4
K_PASS = P * PACK
PASSES = K // K_PASS
HALVES = N // P
QUADRANT = 32
PLANE_ROWS = 4
PASS_ROWS = PLANE_ROWS * P // QUADRANT
LIST_ROWS = 16
BANK = 512
CHUNKS = S // BANK
ALIGN = 256
RUN = 4

W_LATE_AT = 0
SIDE0_AT = PACK * N * 4
SCALE_TABLE_AT = SIDE0_AT - T // 2
WORDS0_AT = SIDE0_AT + T * 4

VECTOR_SHARE = [(576, 1024), (640, 1024)]
PIECES = [
    [(0, 256), (256, 512), (576, 832), (832, 1024), (512, 576)],
    [(0, 256), (256, 512), (640, 832), (832, 1024), (512, 640)],
]
STORES = [
    {512: slice(0, 1024)},
    {0: slice(0, 256), 256: slice(256, 512), 640: slice(640, 832), 832: slice(832, 1024), 512: slice(512, 640)},
]


def tile_picked_sidegate_sigmoid_p_kernel(tc, x_words, x_scales, side, w1, offs, out):
    nc = tc.nc
    with ExitStack() as ctx:
        keep = ctx.enter_context(tc.tile_pool(name="keep", bufs=1))
        reused = ctx.enter_context(tc.tile_pool(name="reused", bufs=1))
        psum = ctx.enter_context(tc.psum_pool(name="psum", bufs=1))

        offsets = keep.tile([P, S // LIST_ROWS], U16, name="offsets")
        scale_table = reused.tile([P, T], U8, name="scale_table", align_bytes=ALIGN, offset=SCALE_TABLE_AT)
        word_table = [
            reused.tile([P, T], I32, name="word_table0", align_bytes=ALIGN, offset=WORDS0_AT),
            keep.tile([P, T], I32, name="word_table1", align_bytes=ALIGN),
        ]
        w_raw = [
            keep.tile([P, PACK, N], F32, name="w_raw0", align_bytes=ALIGN),
            reused.tile([P, PACK, N], F32, name="w_raw1", align_bytes=ALIGN, offset=W_LATE_AT),
        ]
        side_table = [
            reused.tile([P, T], F32, name="side_table0", align_bytes=ALIGN, offset=SIDE0_AT),
            reused.tile([P, T], F32, name="side_table1", align_bytes=ALIGN, offset=WORDS0_AT),
        ]
        scales_picked = keep.tile([P, S], U8, name="scales_picked", align_bytes=ALIGN)
        x_planes = [keep.tile([P, S], U8, name="x_plane%d" % z, align_bytes=ALIGN) for z in range(PASSES)]

        def entries(first, last):
            return offsets[:, first // LIST_ROWS : last // LIST_ROWS]

        def load_words(z):
            nc.sync.dma_start(out=word_table[z][:], in_=x_words[z].rearrange("p c t -> p (c t)").bitcast(I32))

        def load_weights(z, partitions=slice(0, P)):
            rows = w1[z * K_PASS : (z + 1) * K_PASS, :]
            nc.sync.dma_start(out=w_raw[z][partitions], in_=rows.rearrange("(p t) n -> p t n", t=PACK)[partitions])

        def load_side(h):
            nc.sync.dma_start(out=side_table[h][:], in_=side[h * P : (h + 1) * P, :])

        def move_scales(z):
            for r in range(PLANE_ROWS):
                nc.sync.dma_start(
                    out=x_planes[z][PLANE_ROWS * z + r : P : QUADRANT, :].bitcast(I32),
                    in_=scales_picked[PASS_ROWS * z + r : PASS_ROWS * (z + 1) : PLANE_ROWS, :].bitcast(I32),
                )

        def gather_words(z):
            picked = keep.tile([P, S], U32, name="x_codes%d" % z, align_bytes=ALIGN)
            nc.vector.tensor_copy(picked[:], word_table[z][:].bitcast(U32).indirect(offsets[:]))
            return picked

        def quantise_weights(z):
            grouped = keep.tile([P, N, PACK], BF16, name="w_grouped%d" % z, align_bytes=ALIGN)
            nc.scalar.copy(
                out=grouped[:].rearrange("p (c i) t -> p c t i", i=RUN),
                in_=w_raw[z][:].rearrange("p t (c i) -> p c t i", i=RUN),
            )
            codes = keep.tile([P, N], U32, name="w_codes%d" % z, align_bytes=ALIGN)
            plane = keep.tile([P, N], U8, name="w_plane%d" % z, align_bytes=ALIGN)
            nc.vector.quantize_mx(out=codes[:].bitcast(FP8X4), scales=plane[:], in_=grouped[:].rearrange("p n t -> p (n t)"))
            return codes, plane

        banks = [[psum.tile([P, BANK], F32, name="acc%d_%d" % (h, c)) for c in range(CHUNKS)] for h in range(HALVES)]

        def multiply(z, w_codes, w_plane, x_codes):
            for h in range(HALVES):
                for c in range(CHUNKS):
                    nc.tensor.matmul_mx(
                        out=banks[h][c][:],
                        lhsT=w_codes[:, h * P : (h + 1) * P].bitcast(FP8X4),
                        lhsT_scale=w_plane[:, h * P : (h + 1) * P],
                        rhs=x_codes[:, c * BANK : (c + 1) * BANK].bitcast(FP8X4),
                        rhs_scale=x_planes[z][PLANE_ROWS * z : P, c * BANK : (c + 1) * BANK],
                        start=(z == 0),
                        stop=(z == PASSES - 1),
                    )

        def finish(h):
            result = keep.tile([P, S], F32, name="result%d" % h, align_bytes=ALIGN)
            share_first, share_last = VECTOR_SHARE[h]
            side_picked = keep.tile([P, share_last - share_first], F32, name="side_picked%d" % h, align_bytes=ALIGN)
            nc.vector.tensor_copy(side_picked[:], side_table[h][:].indirect(entries(share_first, share_last)))
            for first, last in PIECES[h]:
                gate = keep.tile([P, last - first], F32, name="gate%d_%d" % (h, first), align_bytes=ALIGN)
                if first >= share_first:
                    nc.scalar.activation(gate[:], side_picked[:, first - share_first : last - share_first], SIGMOID)
                else:
                    nc.scalar.activation(gate[:], side_table[h][:].indirect(entries(first, last)), SIGMOID)
                product = banks[h][first // BANK][:, first % BANK : first % BANK + last - first]
                nc.vector.tensor_tensor(result[:, first:last], product, gate[:], MULT)
                if first in STORES[h]:
                    stored = STORES[h][first]
                    nc.sync.dma_start(out=out[h * P : (h + 1) * P, stored], in_=result[:, stored])

        nc.vector.memset(scale_table[QUADRANT : 2 * QUADRANT, :].bitcast(I32), 0)
        nc.vector.memset(scale_table[2 * QUADRANT : P, :].bitcast(I32), 0)
        load_weights(0, slice(0, P, 4))
        nc.sync.dma_start(
            out=scale_table[0 : PASSES * PASS_ROWS, :].bitcast(I32),
            in_=x_scales.rearrange("z g c -> (z g) c").bitcast(I32),
        )
        nc.sync.dma_start(offsets[:], offs)
        load_words(0)
        load_weights(0, slice(1, P, 2))
        load_weights(0, slice(2, P, 4))
        load_words(1)

        warm = keep.tile([P, 8], F32, name="warm")
        nc.vector.memset(warm[:, 0:4], 0.0)
        nc.scalar.activation(warm[:, 4:5], warm[:, 0:1], SIGMOID)

        nc.vector.tensor_copy(scales_picked[:], scale_table[:].indirect(offsets[:]))
        x_codes0 = gather_words(0)
        move_scales(0)
        load_weights(1)
        load_side(0)
        move_scales(1)
        load_side(1)

        w_codes0, w_plane0 = quantise_weights(0)
        x_codes1 = gather_words(1)
        w_codes1, w_plane1 = quantise_weights(1)
        multiply(0, w_codes0, w_plane0, x_codes0)
        multiply(1, w_codes1, w_plane1, x_codes1)
        for h in range(HALVES):
            finish(h)
